import numpy as np
import ml_dtypes


def mxq(x, axis, fmt="e4m3"):
    dtype, down = {"e4m3": (ml_dtypes.float8_e4m3fn, 7), "e5m2": (ml_dtypes.float8_e5m2, 14)}[fmt]
    v = np.moveaxis(np.asarray(x, np.float32).astype(ml_dtypes.bfloat16).astype(np.float64), axis, -1)
    blocks = v.reshape(v.shape[:-1] + (-1, 32))
    amax = np.abs(blocks).max(-1, keepdims=True)
    byte = np.maximum(np.where(amax > 0, np.frexp(amax)[1] - 1 + 127, 0) - down, 1)
    scale = np.exp2(byte - 127.0)
    codes = (blocks / scale).astype(np.float32).astype(dtype).astype(np.float64)
    return np.moveaxis((codes * scale).reshape(v.shape), -1, axis)


WIDE = False


def mx_kscale(k, group=512):
    if not WIDE:
        return np.ones(k)
    levels = np.array([18, -18])
    if group != 512:
        return np.exp2(np.random.permutation(np.resize(levels, k // group))).repeat(group)
    if k % 512:
        return np.exp2(np.random.permutation(np.resize(levels, k // 32))).repeat(32)
    a = np.empty((k // 512, 16))
    for p in range(k // 512):
        a[p, :8] = np.random.permutation(np.resize(levels, 8))
        for g in range(8):
            far = levels[np.abs(levels - a[p, g]) >= 10]
            a[p, g + 8] = far[np.random.randint(len(far))]
    return np.exp2(a.ravel()).repeat(32)


def f64(x):
    return np.asarray(x).astype(np.float64)


def silu(v):
    return v / (1.0 + np.exp(-v))


G, D, M, N = 8, 128, 128, 512


def setup_inputs():
    n = np.random.standard_normal
    s = mx_kscale(D, 0)[:, None]
    return {
        "x": (n((G, D, N)) * s).astype(np.float32),
        "w": (n((G, D, M)) / np.sqrt(D) / s).astype(np.float32),
        "b": (0.5 * n((G, M, 1))).astype(np.float32),
    }


def reference(x, w, b):
    xq = mxq(f64(x), 1, "e4m3")
    y = mxq(f64(w), 1, "e4m3").transpose(0, 2, 1) @ xq
    y = y + f64(b)
    y = silu(y)
    return y

@@ -1,0 +1,122 @@
+from contextlib import ExitStack
+
+import concourse.mybir as mybir
+
+G, D, M, N = 8, 128, 128, 512
+FLOPS = 2 * G * D * M * N
+
+F32 = mybir.dt.float32
+BF16 = mybir.dt.bfloat16
+U32 = mybir.dt.uint32
+U8 = mybir.dt.uint8
+FP8X4 = mybir.dt.float8_e4m3fn_x4
+SILU = mybir.ActivationFunctionType.Silu
+
+P = 128
+PACK = 4
+ROWS = D // PACK
+SIDE = P // ROWS
+SETS = G // SIDE
+CHUNK = 256
+PIECE = 128
+BLK = 32
+
+
+def tile_rows_glin_silu_bias_kernel(tc, x, w, b, out):
+    nc = tc.nc
+    chunks = [(s, n0) for s in range(SETS) for n0 in range(0, N, CHUNK)]
+
+    with ExitStack() as ctx:
+        sb = ctx.enter_context(tc.tile_pool(name="sb", bufs=1))
+        psum = ctx.enter_context(tc.psum_pool(name="psum", bufs=1))
+        ctx.enter_context(tc.manual_schedule())
+
+        b_rows = sb.tile([P, G * BLK], F32, name="b_rows", align_bytes=64)
+        b_cols = sb.tile([P, G * BLK], F32, name="b_cols", align_bytes=64)
+        warm_in = sb.tile([P, 1], F32, name="warm_in")
+        warm_out = sb.tile([P, 1], F32, name="warm_out")
+        nc.vector.memset(b_rows[:], 0.0)
+        nc.vector.memset(warm_in[:], 0.0)
+        nc.scalar.dma_start(
+            out=b_rows[0:P:BLK, :].rearrange("q (g i) -> q g i", i=BLK),
+            in_=b.rearrange("g (q i) o -> q g (i o)", i=BLK),
+        )
+        nc.scalar.activation(out=warm_out[:], in_=warm_in[:], func=SILU)
+
+        def load(src, width, name):
+            raw = sb.tile([P, PACK, width], F32, name=name, align_bytes=64)
+            nc.sync.dma_start(out=raw[:], in_=src.rearrange("g (p j) n -> (g p) j n", j=PACK))
+            return raw
+
+        w_raw = {}
+        x_raw = {}
+        for s, n0 in chunks:
+            groups = slice(s * SIDE, (s + 1) * SIDE)
+            if n0 == 0:
+                w_raw[s] = load(w[groups], M, "w_raw%d" % s)
+            x_raw[s, n0] = load(x[groups, :, n0 : n0 + CHUNK], CHUNK, "x_raw%d_%d" % (s, n0))
+
+        def interleave(raw, c0, name):
+            grouped = sb.tile([P, PIECE, PACK], BF16, name=name, align_bytes=64)
+            nc.vector.tensor_copy(
+                out=grouped[:].rearrange("p (c i) j -> p c j i", i=4),
+                in_=raw[:, :, c0 : c0 + PIECE].rearrange("p j (c i) -> p c j i", i=4),
+            )
+            return grouped
+
+        def quantize(grouped, name):
+            codes = sb.tile([P, PIECE], U32, name=name + "_codes", align_bytes=64)
+            scales = sb.tile([P, PIECE], U8, name=name + "_scales", align_bytes=64)
+            nc.vector.quantize_mx(
+                out=codes[:].bitcast(FP8X4),
+                scales=scales[:],
+                in_=grouped[:].rearrange("p c j -> p (c j)"),
+            )
+            return codes, scales
+
+        banks = [[psum.tile([P, N], F32, name="bank%d_%d" % (h, c)) for c in range(SIDE)] for h in range(2)]
+        y0 = [sb.tile([P, N], F32, name="y0_%d" % c) for c in range(SIDE)]
+        y1 = [sb.tile([P, SIDE, CHUNK], F32, name="y1_%d" % h) for h in range(2)]
+
+        w_q = {}
+        for s, n0 in chunks:
+            h = n0 // CHUNK
+            if n0 == 0:
+                wg = interleave(w_raw[s], 0, "w_g%d" % s)
+                if s == 0:
+                    nc.vector.transpose(out=b_cols[:], in_=b_rows[:])
+                    w_q[s] = quantize(wg, "w%d" % s)
+            xg = [interleave(x_raw[s, n0], u * PIECE, "x_g%d_%d_%d" % (s, n0, u)) for u in range(2)]
+            if n0 == 0 and s == 1:
+                w_q[s] = quantize(wg, "w%d" % s)
+            for u in range(2):
+                x_codes, x_scales = quantize(xg[u], "x%d_%d_%d" % (s, n0, u))
+                w_codes, w_scales = w_q[s]
+                for c in range(SIDE):
+                    rows = slice(c * ROWS, (c + 1) * ROWS)
+                    col = s * CHUNK + u * PIECE
+                    nc.tensor.matmul_mx(
+                        out=banks[h][c][:, col : col + PIECE],
+                        lhsT=w_codes[rows, :].bitcast(FP8X4),
+                        lhsT_scale=w_scales[rows, :],
+                        rhs=x_codes[rows, :].bitcast(FP8X4),
+                        rhs_scale=x_scales[rows, :],
+                        start=True,
+                        stop=True,
+                    )
+            for c in range(SIDE):
+                g = s * SIDE + c
+                dst = y0[c][:, n0 : n0 + CHUNK] if s == 0 else y1[h][:, c, :]
+                nc.scalar.activation(
+                    out=dst,
+                    in_=banks[h][c][:, s * CHUNK : (s + 1) * CHUNK],
+                    func=SILU,
+                    bias=b_cols[:, g * BLK : g * BLK + 1],
+                )
+                if s == 0 and h == 1:
+                    nc.sync.dma_start(out=out[g], in_=y0[c][:])
+                if s == 1 and c % 2 == 1:
+                    nc.sync.dma_start(
+                        out=out[g - 1 : g + 1, :, n0 : n0 + CHUNK].rearrange("g m n -> m g n"),
+                        in_=y1[h][:, c - 1 : c + 1, :],
+                    )

@@ -17,14 +17,14 @@ PACK = 4
 ROWS = D // PACK
 SIDE = P // ROWS
 SETS = G // SIDE
-CHUNK = 256
-PIECE = 128
+MM_N = 128
 BLK = 32
+CHUNKS = [[0,0,256],[0,256,256],[1,0,256],[1,256,256]]
+STORES = {(0, 1): (0, 0, 256), (0, 3): (2, 0, 256), (1, 1): (0, 256, 512), (1, 3): (2, 256, 512), (2, 1): (0, 0, 256), (2, 3): (2, 0, 256), (3, 1): (0, 256, 512), (3, 3): (2, 256, 512)}
 
 
 def tile_rows_glin_silu_bias_kernel(tc, x, w, b, out):
     nc = tc.nc
-    chunks = [(s, n0) for s in range(SETS) for n0 in range(0, N, CHUNK)]
 
     with ExitStack() as ctx:
         sb = ctx.enter_context(tc.tile_pool(name="sb", bufs=1))
@@ -35,12 +35,8 @@ def tile_rows_glin_silu_bias_kernel(tc, x, w, b, out):
         b_cols = sb.tile([P, G * BLK], F32, name="b_cols", align_bytes=64)
         warm_in = sb.tile([P, 1], F32, name="warm_in")
         warm_out = sb.tile([P, 1], F32, name="warm_out")
-        nc.vector.memset(b_rows[:], 0.0)
         nc.vector.memset(warm_in[:], 0.0)
-        nc.scalar.dma_start(
-            out=b_rows[0:P:BLK, :].rearrange("q (g i) -> q g i", i=BLK),
-            in_=b.rearrange("g (q i) o -> q g (i o)", i=BLK),
-        )
+        nc.vector.memset(b_rows[:], 0.0)
         nc.scalar.activation(out=warm_out[:], in_=warm_in[:], func=SILU)
 
         def load(src, width, name):
@@ -49,74 +45,82 @@ def tile_rows_glin_silu_bias_kernel(tc, x, w, b, out):
             return raw
 
         w_raw = {}
-        x_raw = {}
-        for s, n0 in chunks:
+        x_raw = []
+        for k, (s, n0, width) in enumerate(CHUNKS):
             groups = slice(s * SIDE, (s + 1) * SIDE)
-            if n0 == 0:
+            if s not in w_raw:
                 w_raw[s] = load(w[groups], M, "w_raw%d" % s)
-            x_raw[s, n0] = load(x[groups, :, n0 : n0 + CHUNK], CHUNK, "x_raw%d_%d" % (s, n0))
+            x_raw.append(load(x[groups, :, n0 : n0 + width], width, "x_raw%d" % k))
+            if k == 0:
+                nc.sync.dma_start(
+                    out=b_rows[0:P:BLK, :].rearrange("q (g i) -> q g i", i=BLK),
+                    in_=b.rearrange("g (q i) o -> q g (i o)", i=BLK),
+                )
 
-        def interleave(raw, c0, name):
-            grouped = sb.tile([P, PIECE, PACK], BF16, name=name, align_bytes=64)
+        def interleave(raw, c0, width, name):
+            grouped = sb.tile([P, width, PACK], BF16, name=name, align_bytes=64)
             nc.vector.tensor_copy(
                 out=grouped[:].rearrange("p (c i) j -> p c j i", i=4),
-                in_=raw[:, :, c0 : c0 + PIECE].rearrange("p j (c i) -> p c j i", i=4),
+                in_=raw[:, :, c0 : c0 + width].rearrange("p j (c i) -> p c j i", i=4),
             )
             return grouped
 
-        def quantize(grouped, name):
-            codes = sb.tile([P, PIECE], U32, name=name + "_codes", align_bytes=64)
-            scales = sb.tile([P, PIECE], U8, name=name + "_scales", align_bytes=64)
-            nc.vector.quantize_mx(
-                out=codes[:].bitcast(FP8X4),
-                scales=scales[:],
-                in_=grouped[:].rearrange("p c j -> p (c j)"),
-            )
+        def operand(width, name):
+            codes = sb.tile([P, width], U32, name=name + "_codes", align_bytes=64)
+            scales = sb.tile([P, width], U8, name=name + "_scales", align_bytes=64)
             return codes, scales
 
+        def quantize(grouped, dst, c0, width):
+            nc.vector.quantize_mx(
+                out=dst[0][:, c0 : c0 + width].bitcast(FP8X4),
+                scales=dst[1][:, c0 : c0 + width],
+                in_=grouped[:].rearrange("p c j -> p (c j)"),
+            )
+
         banks = [[psum.tile([P, N], F32, name="bank%d_%d" % (h, c)) for c in range(SIDE)] for h in range(2)]
-        y0 = [sb.tile([P, N], F32, name="y0_%d" % c) for c in range(SIDE)]
-        y1 = [sb.tile([P, SIDE, CHUNK], F32, name="y1_%d" % h) for h in range(2)]
+        y = [sb.tile([P, SIDE, N], F32, name="y%d" % s) for s in range(SETS)]
 
         w_q = {}
-        for s, n0 in chunks:
-            h = n0 // CHUNK
-            if n0 == 0:
-                wg = interleave(w_raw[s], 0, "w_g%d" % s)
-                if s == 0:
-                    nc.vector.transpose(out=b_cols[:], in_=b_rows[:])
-                    w_q[s] = quantize(wg, "w%d" % s)
-            xg = [interleave(x_raw[s, n0], u * PIECE, "x_g%d_%d_%d" % (s, n0, u)) for u in range(2)]
-            if n0 == 0 and s == 1:
-                w_q[s] = quantize(wg, "w%d" % s)
+        for k, (s, n0, width) in enumerate(CHUNKS):
+            bank = banks[k % 2]
+            half = width // 2
+            first = s not in w_q
+            if first:
+                w_q[s] = operand(M, "w%d" % s)
+                wg = [interleave(w_raw[s], u * 64, 64, "w_g%d_%d" % (s, u)) for u in range(2)]
+                for u in range(2):
+                    quantize(wg[u], w_q[s], u * 64, 64)
+            xq = operand(width, "x%d" % k)
+            xg = [interleave(x_raw[k], u * half, half, "x_g%d_%d" % (k, u)) for u in range(2)]
             for u in range(2):
-                x_codes, x_scales = quantize(xg[u], "x%d_%d_%d" % (s, n0, u))
-                w_codes, w_scales = w_q[s]
-                for c in range(SIDE):
-                    rows = slice(c * ROWS, (c + 1) * ROWS)
-                    col = s * CHUNK + u * PIECE
-                    nc.tensor.matmul_mx(
-                        out=banks[h][c][:, col : col + PIECE],
-                        lhsT=w_codes[rows, :].bitcast(FP8X4),
-                        lhsT_scale=w_scales[rows, :],
-                        rhs=x_codes[rows, :].bitcast(FP8X4),
-                        rhs_scale=x_scales[rows, :],
-                        start=True,
-                        stop=True,
-                    )
+                quantize(xg[u], xq, u * half, half)
+            if k == 0:
+                nc.vector.transpose(out=b_cols[:], in_=b_rows[:])
+            for c0 in range(0, SIDE, 2):
+                for col in range(0, width, MM_N):
+                    for c in (c0, c0 + 1):
+                        rows = slice(c * ROWS, (c + 1) * ROWS)
+                        cols = slice(col, col + MM_N)
+                        nc.tensor.matmul_mx(
+                            out=bank[c][:, cols],
+                            lhsT=w_q[s][0][rows, :].bitcast(FP8X4),
+                            lhsT_scale=w_q[s][1][rows, :],
+                            rhs=xq[0][rows, cols].bitcast(FP8X4),
+                            rhs_scale=xq[1][rows, cols],
+                            start=True,
+                            stop=True,
+                        )
             for c in range(SIDE):
                 g = s * SIDE + c
-                dst = y0[c][:, n0 : n0 + CHUNK] if s == 0 else y1[h][:, c, :]
                 nc.scalar.activation(
-                    out=dst,
-                    in_=banks[h][c][:, s * CHUNK : (s + 1) * CHUNK],
+                    out=y[s][:, c, n0 : n0 + width],
+                    in_=bank[c][:, 0:width],
                     func=SILU,
                     bias=b_cols[:, g * BLK : g * BLK + 1],
                 )
-                if s == 0 and h == 1:
-                    nc.sync.dma_start(out=out[g], in_=y0[c][:])
-                if s == 1 and c % 2 == 1:
+                if (k, c) in STORES:
+                    c_lo, n_lo, n_hi = STORES[k, c]
                     nc.sync.dma_start(
-                        out=out[g - 1 : g + 1, :, n0 : n0 + CHUNK].rearrange("g m n -> m g n"),
-                        in_=y1[h][:, c - 1 : c + 1, :],
+                        out=out[s * SIDE + c_lo : g + 1, :, n_lo:n_hi].rearrange("g m n -> m g n"),
+                        in_=y[s][:, c_lo : c + 1, n_lo:n_hi],
                     )

@@ -20,7 +20,7 @@ SETS = G // SIDE
 MM_N = 128
 BLK = 32
 CHUNKS = [[0,0,256],[0,256,256],[1,0,256],[1,256,256]]
-STORES = {(0, 1): (0, 0, 256), (0, 3): (2, 0, 256), (1, 1): (0, 256, 512), (1, 3): (2, 256, 512), (2, 1): (0, 0, 256), (2, 3): (2, 0, 256), (3, 1): (0, 256, 512), (3, 3): (2, 256, 512)}
+STORES = {(0, 1): (0, 0, 256), (0, 3): (2, 0, 256), (1, 1): (0, 256, 512), (1, 3): (2, 256, 512), (2, 1): (0, 0, 256), (2, 3): (2, 0, 256), (3, 1): (0, 256, 512), (3, 2): (2, 256, 512), (3, 3): (3, 256, 512)}
 
 
 def tile_rows_glin_silu_bias_kernel(tc, x, w, b, out):
@@ -35,8 +35,8 @@ def tile_rows_glin_silu_bias_kernel(tc, x, w, b, out):
         b_cols = sb.tile([P, G * BLK], F32, name="b_cols", align_bytes=64)
         warm_in = sb.tile([P, 1], F32, name="warm_in")
         warm_out = sb.tile([P, 1], F32, name="warm_out")
-        nc.vector.memset(warm_in[:], 0.0)
         nc.vector.memset(b_rows[:], 0.0)
+        nc.vector.memset(warm_in[:], 0.0)
         nc.scalar.activation(out=warm_out[:], in_=warm_in[:], func=SILU)
 
         def load(src, width, name):
@@ -50,12 +50,12 @@ def tile_rows_glin_silu_bias_kernel(tc, x, w, b, out):
             groups = slice(s * SIDE, (s + 1) * SIDE)
             if s not in w_raw:
                 w_raw[s] = load(w[groups], M, "w_raw%d" % s)
-            x_raw.append(load(x[groups, :, n0 : n0 + width], width, "x_raw%d" % k))
             if k == 0:
                 nc.sync.dma_start(
                     out=b_rows[0:P:BLK, :].rearrange("q (g i) -> q g i", i=BLK),
                     in_=b.rearrange("g (q i) o -> q g (i o)", i=BLK),
                 )
+            x_raw.append(load(x[groups, :, n0 : n0 + width], width, "x_raw%d" % k))
 
         def interleave(raw, c0, width, name):
             grouped = sb.tile([P, width, PACK], BF16, name=name, align_bytes=64)
@@ -84,18 +84,20 @@ def tile_rows_glin_silu_bias_kernel(tc, x, w, b, out):
         for k, (s, n0, width) in enumerate(CHUNKS):
             bank = banks[k % 2]
             half = width // 2
-            first = s not in w_q
-            if first:
-                w_q[s] = operand(M, "w%d" % s)
-                wg = [interleave(w_raw[s], u * 64, 64, "w_g%d_%d" % (s, u)) for u in range(2)]
-                for u in range(2):
-                    quantize(wg[u], w_q[s], u * 64, 64)
+            if k == 0:
+                w_q[0] = operand(M, "w0")
+                wg = interleave(w_raw[0], 0, M, "w_g0")
+                nc.vector.transpose(out=b_cols[:], in_=b_rows[:])
+                quantize(wg, w_q[0], 0, M)
             xq = operand(width, "x%d" % k)
             xg = [interleave(x_raw[k], u * half, half, "x_g%d_%d" % (k, u)) for u in range(2)]
-            for u in range(2):
-                quantize(xg[u], xq, u * half, half)
-            if k == 0:
-                nc.vector.transpose(out=b_cols[:], in_=b_rows[:])
+            quantize(xg[0], xq, 0, half)
+            if k == 1:
+                w_q[1] = operand(M, "w1")
+                wg = interleave(w_raw[1], 0, M, "w_g1")
+            quantize(xg[1], xq, half, half)
+            if k == 1:
+                quantize(wg, w_q[1], 0, M)
             for c0 in range(0, SIDE, 2):
                 for col in range(0, width, MM_N):
                     for c in (c0, c0 + 1):

@@ -19,8 +19,8 @@ SIDE = P // ROWS
 SETS = G // SIDE
 MM_N = 128
 BLK = 32
-CHUNKS = [[0,0,256],[0,256,256],[1,0,256],[1,256,256]]
-STORES = {(0, 1): (0, 0, 256), (0, 3): (2, 0, 256), (1, 1): (0, 256, 512), (1, 3): (2, 256, 512), (2, 1): (0, 0, 256), (2, 3): (2, 0, 256), (3, 1): (0, 256, 512), (3, 2): (2, 256, 512), (3, 3): (3, 256, 512)}
+HALF = N // 2
+RUN = 4
 
 
 def tile_rows_glin_silu_bias_kernel(tc, x, w, b, out):
@@ -31,98 +31,114 @@ def tile_rows_glin_silu_bias_kernel(tc, x, w, b, out):
         psum = ctx.enter_context(tc.psum_pool(name="psum", bufs=1))
         ctx.enter_context(tc.manual_schedule())
 
-        b_rows = sb.tile([P, G * BLK], F32, name="b_rows", align_bytes=64)
-        b_cols = sb.tile([P, G * BLK], F32, name="b_cols", align_bytes=64)
-        warm_in = sb.tile([P, 1], F32, name="warm_in")
-        warm_out = sb.tile([P, 1], F32, name="warm_out")
+        b_rows = sb.tile([P, BLK], F32, name="b_rows", align_bytes=64)
+        b_cols = sb.tile([P, BLK], F32, name="b_cols", align_bytes=64)
+        b_step = BLK // G
         nc.vector.memset(b_rows[:], 0.0)
-        nc.vector.memset(warm_in[:], 0.0)
-        nc.scalar.activation(out=warm_out[:], in_=warm_in[:], func=SILU)
 
-        def load(src, width, name):
-            raw = sb.tile([P, PACK, width], F32, name=name, align_bytes=64)
+        def load(src, name):
+            raw = sb.tile([P, PACK, src.shape[2]], F32, name=name, align_bytes=64)
             nc.sync.dma_start(out=raw[:], in_=src.rearrange("g (p j) n -> (g p) j n", j=PACK))
             return raw
 
-        w_raw = {}
-        x_raw = []
-        for k, (s, n0, width) in enumerate(CHUNKS):
-            groups = slice(s * SIDE, (s + 1) * SIDE)
-            if s not in w_raw:
-                w_raw[s] = load(w[groups], M, "w_raw%d" % s)
-            if k == 0:
-                nc.sync.dma_start(
-                    out=b_rows[0:P:BLK, :].rearrange("q (g i) -> q g i", i=BLK),
-                    in_=b.rearrange("g (q i) o -> q g (i o)", i=BLK),
-                )
-            x_raw.append(load(x[groups, :, n0 : n0 + width], width, "x_raw%d" % k))
+        def load_bias(queue):
+            queue.dma_start(out=b_rows[0:P:b_step, :], in_=b.rearrange("g (q i) o -> q g (i o)", i=BLK))
 
-        def interleave(raw, c0, width, name):
+        def interleave(copy, raw, c0, width, name):
             grouped = sb.tile([P, width, PACK], BF16, name=name, align_bytes=64)
-            nc.vector.tensor_copy(
-                out=grouped[:].rearrange("p (c i) j -> p c j i", i=4),
-                in_=raw[:, :, c0 : c0 + width].rearrange("p j (c i) -> p c j i", i=4),
+            copy(
+                out=grouped[:].rearrange("p (c i) j -> p c j i", i=RUN),
+                in_=raw[:, :, c0 : c0 + width].rearrange("p j (c i) -> p c j i", i=RUN),
             )
             return grouped
 
-        def operand(width, name):
+        def quantize(grouped, name):
+            width = grouped.shape[1]
             codes = sb.tile([P, width], U32, name=name + "_codes", align_bytes=64)
             scales = sb.tile([P, width], U8, name=name + "_scales", align_bytes=64)
-            return codes, scales
-
-        def quantize(grouped, dst, c0, width):
             nc.vector.quantize_mx(
-                out=dst[0][:, c0 : c0 + width].bitcast(FP8X4),
-                scales=dst[1][:, c0 : c0 + width],
-                in_=grouped[:].rearrange("p c j -> p (c j)"),
+                out=codes[:].bitcast(FP8X4), scales=scales[:], in_=grouped[:].rearrange("p c j -> p (c j)")
             )
+            return [(codes, scales, c0) for c0 in range(0, width, MM_N)]
 
         banks = [[psum.tile([P, N], F32, name="bank%d_%d" % (h, c)) for c in range(SIDE)] for h in range(2)]
         y = [sb.tile([P, SIDE, N], F32, name="y%d" % s) for s in range(SETS)]
 
-        w_q = {}
-        for k, (s, n0, width) in enumerate(CHUNKS):
-            bank = banks[k % 2]
-            half = width // 2
-            if k == 0:
-                w_q[0] = operand(M, "w0")
-                wg = interleave(w_raw[0], 0, M, "w_g0")
-                nc.vector.transpose(out=b_cols[:], in_=b_rows[:])
-                quantize(wg, w_q[0], 0, M)
-            xq = operand(width, "x%d" % k)
-            xg = [interleave(x_raw[k], u * half, half, "x_g%d_%d" % (k, u)) for u in range(2)]
-            quantize(xg[0], xq, 0, half)
-            if k == 1:
-                w_q[1] = operand(M, "w1")
-                wg = interleave(w_raw[1], 0, M, "w_g1")
-            quantize(xg[1], xq, half, half)
-            if k == 1:
-                quantize(wg, w_q[1], 0, M)
-            for c0 in range(0, SIDE, 2):
-                for col in range(0, width, MM_N):
-                    for c in (c0, c0 + 1):
-                        rows = slice(c * ROWS, (c + 1) * ROWS)
-                        cols = slice(col, col + MM_N)
-                        nc.tensor.matmul_mx(
-                            out=bank[c][:, cols],
-                            lhsT=w_q[s][0][rows, :].bitcast(FP8X4),
-                            lhsT_scale=w_q[s][1][rows, :],
-                            rhs=xq[0][rows, cols].bitcast(FP8X4),
-                            rhs_scale=xq[1][rows, cols],
-                            start=True,
-                            stop=True,
-                        )
-            for c in range(SIDE):
-                g = s * SIDE + c
-                nc.scalar.activation(
-                    out=y[s][:, c, n0 : n0 + width],
-                    in_=bank[c][:, 0:width],
-                    func=SILU,
-                    bias=b_cols[:, g * BLK : g * BLK + 1],
-                )
-                if (k, c) in STORES:
-                    c_lo, n_lo, n_hi = STORES[k, c]
-                    nc.sync.dma_start(
-                        out=out[s * SIDE + c_lo : g + 1, :, n_lo:n_hi].rearrange("g m n -> m g n"),
-                        in_=y[s][:, c_lo : c + 1, n_lo:n_hi],
+        def multiply(w_q, x_q, bank, places):
+            w_codes, w_scales, unused = w_q[0]
+            for c in places:
+                for u, (codes, scales, c0) in enumerate(x_q):
+                    rows = slice(c * ROWS, (c + 1) * ROWS)
+                    nc.tensor.matmul_mx(
+                        out=bank[c][:, u * MM_N : (u + 1) * MM_N],
+                        lhsT=w_codes[rows, :].bitcast(FP8X4),
+                        lhsT_scale=w_scales[rows, :],
+                        rhs=codes[rows, c0 : c0 + MM_N].bitcast(FP8X4),
+                        rhs_scale=scales[rows, c0 : c0 + MM_N],
+                        start=True,
+                        stop=True,
                     )
+
+        def activate(s, c, bank, n0, width):
+            g = s * SIDE + c
+            nc.scalar.activation(
+                out=y[s][:, c, n0 : n0 + width],
+                in_=bank[c][:, 0:width],
+                func=SILU,
+                bias=b_cols[:, g * b_step : g * b_step + 1],
+            )
+
+        def store(s, c_lo, c_hi, n0, width):
+            nc.sync.dma_start(
+                out=out[s * SIDE + c_lo : s * SIDE + c_hi, :, n0 : n0 + width].rearrange("g m n -> m g n"),
+                in_=y[s][:, c_lo:c_hi, n0 : n0 + width],
+            )
+
+        on_vector = nc.vector.tensor_copy
+        on_scalar = nc.scalar.copy
+
+        warm_in = sb.tile([P, 1], F32, name="warm_in")
+        warm_out = sb.tile([P, 1], F32, name="warm_out")
+        nc.vector.memset(warm_in[:], 0.0)
+        nc.scalar.activation(out=warm_out[:], in_=warm_in[:], func=SILU)
+
+        w_raw0 = load(w[0:SIDE], "w_raw0")
+        x_raw = {(0, 0): load(x[0:SIDE, :, 0:HALF], "x_raw0_0")}
+        load_bias(nc.sync)
+        x_raw[0, 1] = load(x[0:SIDE, :, HALF:N], "x_raw0_1")
+        x_raw[1, 0] = load(x[SIDE:G, :, 0:HALF], "x_raw1_0")
+        w_raw1 = load(w[SIDE:G], "w_raw1")
+        x_raw[1, 1] = load(x[SIDE:G, :, HALF:N], "x_raw1_1")
+
+        def finish(s, h, w_q, x_q, bank, n0, stores):
+            multiply(w_q, x_q, bank, range(SIDE))
+            for c in range(SIDE):
+                activate(s, c, bank, n0, MM_N * len(x_q))
+                if stores and s == SETS - 1 and h == 1 and c >= 2:
+                    store(s, c, c + 1, h * HALF, HALF)
+                elif stores and c % 2 == 1:
+                    store(s, c - 1, c + 1, h * HALF, HALF)
+
+        def piece(copy, s, h, u):
+            return interleave(copy, x_raw[s, h], u * MM_N, MM_N, "x_g%d_%d_%d" % (s, h, u))
+
+        w_q0 = quantize(interleave(on_vector, w_raw0, 0, M, "w_g0"), "w0")
+        part = [piece(on_vector, 0, 0, 0), piece(on_scalar, 0, 0, 1)]
+        nc.vector.transpose(out=b_cols[:], in_=b_rows[:])
+        x_q = quantize(part[0], "x00_0") + quantize(part[1], "x00_1")
+        finish(0, 0, w_q0, x_q, banks[0], 0, True)
+
+        part = [piece(on_vector, 0, 1, u) for u in range(2)]
+        x_q = quantize(part[0], "x01_0") + quantize(part[1], "x01_1")
+        finish(0, 1, w_q0, x_q, banks[1], HALF, True)
+
+        part = [piece(on_vector, 1, 0, u) for u in range(2)]
+        w_g1 = interleave(on_vector, w_raw1, 0, M, "w_g1")
+        x_q = quantize(part[0], "x10_0")
+        w_q1 = quantize(w_g1, "w1")
+        x_q = x_q + quantize(part[1], "x10_1")
+        finish(1, 0, w_q1, x_q, banks[0], 0, True)
+
+        part = [piece(on_vector, 1, 1, u) for u in range(2)]
+        x_q = quantize(part[0], "x11_0") + quantize(part[1], "x11_1")
+        finish(1, 1, w_q1, x_q, banks[1], HALF, True)

@@ -95,50 +95,49 @@ def tile_rows_glin_silu_bias_kernel(tc, x, w, b, out):
             )
 
         on_vector = nc.vector.tensor_copy
-        on_scalar = nc.scalar.copy
 
         warm_in = sb.tile([P, 1], F32, name="warm_in")
         warm_out = sb.tile([P, 1], F32, name="warm_out")
         nc.vector.memset(warm_in[:], 0.0)
         nc.scalar.activation(out=warm_out[:], in_=warm_in[:], func=SILU)
 
-        w_raw0 = load(w[0:SIDE], "w_raw0")
         x_raw = {(0, 0): load(x[0:SIDE, :, 0:HALF], "x_raw0_0")}
+        w_raw0 = load(w[0:SIDE], "w_raw0")
         load_bias(nc.sync)
         x_raw[0, 1] = load(x[0:SIDE, :, HALF:N], "x_raw0_1")
         x_raw[1, 0] = load(x[SIDE:G, :, 0:HALF], "x_raw1_0")
         w_raw1 = load(w[SIDE:G], "w_raw1")
         x_raw[1, 1] = load(x[SIDE:G, :, HALF:N], "x_raw1_1")
 
-        def finish(s, h, w_q, x_q, bank, n0, stores):
-            multiply(w_q, x_q, bank, range(SIDE))
-            for c in range(SIDE):
-                activate(s, c, bank, n0, MM_N * len(x_q))
-                if stores and s == SETS - 1 and h == 1 and c >= 2:
-                    store(s, c, c + 1, h * HALF, HALF)
-                elif stores and c % 2 == 1:
-                    store(s, c - 1, c + 1, h * HALF, HALF)
+        def finish(s, w_q, x_q, bank, n0, places, stores):
+            multiply(w_q, x_q, bank, places)
+            for c in places:
+                activate(s, c, bank, n0, HALF)
+                if c in stores:
+                    store(s, *stores[c])
 
         def piece(copy, s, h, u):
             return interleave(copy, x_raw[s, h], u * MM_N, MM_N, "x_g%d_%d_%d" % (s, h, u))
 
-        w_q0 = quantize(interleave(on_vector, w_raw0, 0, M, "w_g0"), "w0")
-        part = [piece(on_vector, 0, 0, 0), piece(on_scalar, 0, 0, 1)]
+        part = [piece(on_vector, 0, 0, u) for u in range(2)]
+        w_g0 = interleave(on_vector, w_raw0, 0, M, "w_g0")
+        x_q = quantize(part[0], "x00_0")
+        w_q0 = quantize(w_g0, "w0")
+        x_q = x_q + quantize(part[1], "x00_1")
         nc.vector.transpose(out=b_cols[:], in_=b_rows[:])
-        x_q = quantize(part[0], "x00_0") + quantize(part[1], "x00_1")
-        finish(0, 0, w_q0, x_q, banks[0], 0, True)
+        finish(0, w_q0, x_q, banks[0], 0, (0, 1, 2, 3), {1: (0, 2, 0, HALF)})
 
         part = [piece(on_vector, 0, 1, u) for u in range(2)]
         x_q = quantize(part[0], "x01_0") + quantize(part[1], "x01_1")
-        finish(0, 1, w_q0, x_q, banks[1], HALF, True)
+        finish(0, w_q0, x_q, banks[1], HALF, (2, 3, 0, 1), {3: (2, 4, 0, N), 1: (0, 2, HALF, HALF)})
 
         part = [piece(on_vector, 1, 0, u) for u in range(2)]
         w_g1 = interleave(on_vector, w_raw1, 0, M, "w_g1")
         x_q = quantize(part[0], "x10_0")
         w_q1 = quantize(w_g1, "w1")
         x_q = x_q + quantize(part[1], "x10_1")
-        finish(1, 0, w_q1, x_q, banks[0], 0, True)
+        finish(1, w_q1, x_q, banks[0], 0, (0, 1, 2, 3), {1: (0, 2, 0, HALF), 3: (2, 4, 0, HALF)})
 
         part = [piece(on_vector, 1, 1, u) for u in range(2)]
         x_q = quantize(part[0], "x11_0") + quantize(part[1], "x11_1")
-        finish(1, 1, w_q1, x_q, banks[1], HALF, True)
+        finish(1, w_q1, x_q, banks[1], HALF, (0, 1, 2, 3), {c: (c, c + 1, HALF, HALF) for c in range(SIDE)})

@@ -37,7 +37,7 @@ def tile_rows_glin_silu_bias_kernel(tc, x, w, b, out):
         nc.vector.memset(b_rows[:], 0.0)
 
         def load(src, name):
-            raw = sb.tile([P, PACK, src.shape[2]], F32, name=name, align_bytes=64)
+            raw = sb.tile([P, PACK, src.shape[2]], F32, name=name, align_bytes=256)
             nc.sync.dma_start(out=raw[:], in_=src.rearrange("g (p j) n -> (g p) j n", j=PACK))
             return raw
 
@@ -62,7 +62,7 @@ def tile_rows_glin_silu_bias_kernel(tc, x, w, b, out):
             return [(codes, scales, c0) for c0 in range(0, width, MM_N)]
 
         banks = [[psum.tile([P, N], F32, name="bank%d_%d" % (h, c)) for c in range(SIDE)] for h in range(2)]
-        y = [sb.tile([P, SIDE, N], F32, name="y%d" % s) for s in range(SETS)]
+        y = [sb.tile([P, SIDE, N], F32, name="y%d" % s, align_bytes=256) for s in range(SETS)]
 
         def multiply(w_q, x_q, bank, places):
             w_codes, w_scales, unused = w_q[0]

@@ -96,6 +96,8 @@ def tile_rows_glin_silu_bias_kernel(tc, x, w, b, out):
 
         on_vector = nc.vector.tensor_copy
 
+        load_bias(nc.scalar)
+
         warm_in = sb.tile([P, 1], F32, name="warm_in")
         warm_out = sb.tile([P, 1], F32, name="warm_out")
         nc.vector.memset(warm_in[:], 0.0)
@@ -103,7 +105,6 @@ def tile_rows_glin_silu_bias_kernel(tc, x, w, b, out):
 
         x_raw = {(0, 0): load(x[0:SIDE, :, 0:HALF], "x_raw0_0")}
         w_raw0 = load(w[0:SIDE], "w_raw0")
-        load_bias(nc.sync)
         x_raw[0, 1] = load(x[0:SIDE, :, HALF:N], "x_raw0_1")
         x_raw[1, 0] = load(x[SIDE:G, :, 0:HALF], "x_raw1_0")
         w_raw1 = load(w[SIDE:G], "w_raw1")
@@ -125,11 +126,11 @@ def tile_rows_glin_silu_bias_kernel(tc, x, w, b, out):
         w_q0 = quantize(w_g0, "w0")
         x_q = x_q + quantize(part[1], "x00_1")
         nc.vector.transpose(out=b_cols[:], in_=b_rows[:])
-        finish(0, w_q0, x_q, banks[0], 0, (0, 1, 2, 3), {1: (0, 2, 0, HALF)})
+        finish(0, w_q0, x_q, banks[0], 0, (0, 1, 2, 3), {3: (0, 4, 0, HALF)})
 
         part = [piece(on_vector, 0, 1, u) for u in range(2)]
         x_q = quantize(part[0], "x01_0") + quantize(part[1], "x01_1")
-        finish(0, w_q0, x_q, banks[1], HALF, (2, 3, 0, 1), {3: (2, 4, 0, N), 1: (0, 2, HALF, HALF)})
+        finish(0, w_q0, x_q, banks[1], HALF, (0, 1, 2, 3), {1: (0, 2, HALF, HALF), 3: (2, 4, HALF, HALF)})
 
         part = [piece(on_vector, 1, 0, u) for u in range(2)]
         w_g1 = interleave(on_vector, w_raw1, 0, M, "w_g1")

@@ -36,15 +36,15 @@ def tile_rows_glin_silu_bias_kernel(tc, x, w, b, out):
         b_step = BLK // G
         nc.vector.memset(b_rows[:], 0.0)
 
-        def load(src, name):
+        def load(src, name, queue=nc.sync):
             raw = sb.tile([P, PACK, src.shape[2]], F32, name=name, align_bytes=256)
-            nc.sync.dma_start(out=raw[:], in_=src.rearrange("g (p j) n -> (g p) j n", j=PACK))
+            queue.dma_start(out=raw[:], in_=src.rearrange("g (p j) n -> (g p) j n", j=PACK))
             return raw
 
-        def load_bias(queue):
-            queue.dma_start(out=b_rows[0:P:b_step, :], in_=b.rearrange("g (q i) o -> q g (i o)", i=BLK))
+        def load_x(s, n0, width, queue=nc.sync):
+            return load(x[s * SIDE : (s + 1) * SIDE, :, n0 : n0 + width], "x_raw%d_%d" % (s, n0), queue)
 
-        def interleave(copy, raw, c0, width, name):
+        def interleave(raw, c0, name, copy=nc.vector.tensor_copy, width=MM_N):
             grouped = sb.tile([P, width, PACK], BF16, name=name, align_bytes=64)
             copy(
                 out=grouped[:].rearrange("p (c i) j -> p c j i", i=RUN),
@@ -59,86 +59,77 @@ def tile_rows_glin_silu_bias_kernel(tc, x, w, b, out):
             nc.vector.quantize_mx(
                 out=codes[:].bitcast(FP8X4), scales=scales[:], in_=grouped[:].rearrange("p c j -> p (c j)")
             )
-            return [(codes, scales, c0) for c0 in range(0, width, MM_N)]
+            return codes, scales
 
         banks = [[psum.tile([P, N], F32, name="bank%d_%d" % (h, c)) for c in range(SIDE)] for h in range(2)]
         y = [sb.tile([P, SIDE, N], F32, name="y%d" % s, align_bytes=256) for s in range(SETS)]
 
-        def multiply(w_q, x_q, bank, places):
-            w_codes, w_scales, unused = w_q[0]
-            for c in places:
-                for u, (codes, scales, c0) in enumerate(x_q):
-                    rows = slice(c * ROWS, (c + 1) * ROWS)
-                    nc.tensor.matmul_mx(
-                        out=bank[c][:, u * MM_N : (u + 1) * MM_N],
-                        lhsT=w_codes[rows, :].bitcast(FP8X4),
-                        lhsT_scale=w_scales[rows, :],
-                        rhs=codes[rows, c0 : c0 + MM_N].bitcast(FP8X4),
-                        rhs_scale=scales[rows, c0 : c0 + MM_N],
-                        start=True,
-                        stop=True,
-                    )
+        def multiply(w_q, x_q, c, h, col):
+            rows = slice(c * ROWS, (c + 1) * ROWS)
+            nc.tensor.matmul_mx(
+                out=banks[h][c][:, col : col + MM_N],
+                lhsT=w_q[0][rows, :].bitcast(FP8X4),
+                lhsT_scale=w_q[1][rows, :],
+                rhs=x_q[0][rows, :].bitcast(FP8X4),
+                rhs_scale=x_q[1][rows, :],
+                start=True,
+                stop=True,
+            )
 
-        def activate(s, c, bank, n0, width):
+        def activate(s, c, h, col, n0, width):
             g = s * SIDE + c
             nc.scalar.activation(
                 out=y[s][:, c, n0 : n0 + width],
-                in_=bank[c][:, 0:width],
+                in_=banks[h][c][:, col : col + width],
                 func=SILU,
                 bias=b_cols[:, g * b_step : g * b_step + 1],
             )
 
-        def store(s, c_lo, c_hi, n0, width):
-            nc.sync.dma_start(
+        def store(s, c_lo, c_hi, n0, width, queue=nc.sync):
+            queue.dma_start(
                 out=out[s * SIDE + c_lo : s * SIDE + c_hi, :, n0 : n0 + width].rearrange("g m n -> m g n"),
                 in_=y[s][:, c_lo:c_hi, n0 : n0 + width],
             )
 
-        on_vector = nc.vector.tensor_copy
-
-        load_bias(nc.scalar)
+        nc.scalar.dma_start(out=b_rows[0:P:b_step, :], in_=b.rearrange("g (q i) o -> q g (i o)", i=BLK))
 
         warm_in = sb.tile([P, 1], F32, name="warm_in")
         warm_out = sb.tile([P, 1], F32, name="warm_out")
         nc.vector.memset(warm_in[:], 0.0)
         nc.scalar.activation(out=warm_out[:], in_=warm_in[:], func=SILU)
 
-        x_raw = {(0, 0): load(x[0:SIDE, :, 0:HALF], "x_raw0_0")}
+        x00 = load_x(0, 0, HALF)
         w_raw0 = load(w[0:SIDE], "w_raw0")
-        x_raw[0, 1] = load(x[0:SIDE, :, HALF:N], "x_raw0_1")
-        x_raw[1, 0] = load(x[SIDE:G, :, 0:HALF], "x_raw1_0")
+        x01 = load_x(0, HALF, HALF)
+        x10 = load_x(1, 0, HALF)
         w_raw1 = load(w[SIDE:G], "w_raw1")
-        x_raw[1, 1] = load(x[SIDE:G, :, HALF:N], "x_raw1_1")
+        x11a = load_x(1, HALF, MM_N)
+        x11b = load_x(1, HALF + MM_N, MM_N)
 
-        def finish(s, w_q, x_q, bank, n0, places, stores):
-            multiply(w_q, x_q, bank, places)
-            for c in places:
-                activate(s, c, bank, n0, HALF)
-                if c in stores:
-                    store(s, *stores[c])
+        def finish(s, w_q, x_q, h):
+            for c in range(SIDE):
+                for u in range(2):
+                    multiply(w_q, x_q[u], c, h, u * MM_N)
+            for c in range(SIDE):
+                activate(s, c, h, 0, h * HALF, HALF)
+                store(s, c, c + 1, h * HALF, HALF)
 
-        def piece(copy, s, h, u):
-            return interleave(copy, x_raw[s, h], u * MM_N, MM_N, "x_g%d_%d_%d" % (s, h, u))
+        def first_half(s, raw, w_raw):
+            part = [interleave(raw, u * MM_N, "x_g%d_0_%d" % (s, u)) for u in range(2)]
+            w_g = interleave(w_raw, 0, "w_g%d" % s)
+            x_q = [quantize(part[0], "x%d0_0" % s)]
+            w_q = quantize(w_g, "w%d" % s)
+            x_q.append(quantize(part[1], "x%d0_1" % s))
+            return w_q, x_q
 
-        part = [piece(on_vector, 0, 0, u) for u in range(2)]
-        w_g0 = interleave(on_vector, w_raw0, 0, M, "w_g0")
-        x_q = quantize(part[0], "x00_0")
-        w_q0 = quantize(w_g0, "w0")
-        x_q = x_q + quantize(part[1], "x00_1")
+        def second_half(s, pieces):
+            part = [interleave(raw, c0, "x_g%d_1_%d" % (s, u)) for u, (raw, c0) in enumerate(pieces)]
+            return [quantize(part[u], "x%d1_%d" % (s, u)) for u in range(2)]
+
+        w_q, x_q = first_half(0, x00, w_raw0)
         nc.vector.transpose(out=b_cols[:], in_=b_rows[:])
-        finish(0, w_q0, x_q, banks[0], 0, (0, 1, 2, 3), {3: (0, 4, 0, HALF)})
-
-        part = [piece(on_vector, 0, 1, u) for u in range(2)]
-        x_q = quantize(part[0], "x01_0") + quantize(part[1], "x01_1")
-        finish(0, w_q0, x_q, banks[1], HALF, (0, 1, 2, 3), {1: (0, 2, HALF, HALF), 3: (2, 4, HALF, HALF)})
-
-        part = [piece(on_vector, 1, 0, u) for u in range(2)]
-        w_g1 = interleave(on_vector, w_raw1, 0, M, "w_g1")
-        x_q = quantize(part[0], "x10_0")
-        w_q1 = quantize(w_g1, "w1")
-        x_q = x_q + quantize(part[1], "x10_1")
-        finish(1, w_q1, x_q, banks[0], 0, (0, 1, 2, 3), {1: (0, 2, 0, HALF), 3: (2, 4, 0, HALF)})
-
-        part = [piece(on_vector, 1, 1, u) for u in range(2)]
-        x_q = quantize(part[0], "x11_0") + quantize(part[1], "x11_1")
-        finish(1, w_q1, x_q, banks[1], HALF, (0, 1, 2, 3), {c: (c, c + 1, HALF, HALF) for c in range(SIDE)})
+        finish(0, w_q, x_q, 0)
+        finish(0, w_q, second_half(0, [(x01, 0), (x01, MM_N)]), 1)
+        w_q, x_q = first_half(1, x10, w_raw1)
+        finish(1, w_q, x_q, 0)
+        finish(1, w_q, second_half(1, [(x11a, 0), (x11b, 0)]), 1)

@@ -101,35 +101,34 @@ def tile_rows_glin_silu_bias_kernel(tc, x, w, b, out):
         x00 = load_x(0, 0, HALF)
         w_raw0 = load(w[0:SIDE], "w_raw0")
         x01 = load_x(0, HALF, HALF)
-        x10 = load_x(1, 0, HALF)
         w_raw1 = load(w[SIDE:G], "w_raw1")
-        x11a = load_x(1, HALF, MM_N)
-        x11b = load_x(1, HALF + MM_N, MM_N)
+        x1 = [load_x(1, u * MM_N, MM_N) for u in range(4)]
 
-        def finish(s, w_q, x_q, h):
+        def finish(s, w_q, x_q, h, first_store=0):
             for c in range(SIDE):
                 for u in range(2):
                     multiply(w_q, x_q[u], c, h, u * MM_N)
             for c in range(SIDE):
                 activate(s, c, h, 0, h * HALF, HALF)
-                store(s, c, c + 1, h * HALF, HALF)
+                if c >= first_store:
+                    store(s, c if c > first_store else 0, c + 1, h * HALF, HALF)
 
-        def first_half(s, raw, w_raw):
-            part = [interleave(raw, u * MM_N, "x_g%d_0_%d" % (s, u)) for u in range(2)]
-            w_g = interleave(w_raw, 0, "w_g%d" % s)
-            x_q = [quantize(part[0], "x%d0_0" % s)]
-            w_q = quantize(w_g, "w%d" % s)
-            x_q.append(quantize(part[1], "x%d0_1" % s))
-            return w_q, x_q
+        def pair(s, h, pieces):
+            part = [interleave(raw, c0, "x_g%d_%d_%d" % (s, h, u)) for u, (raw, c0) in enumerate(pieces)]
+            return [quantize(part[u], "x%d%d_%d" % (s, h, u)) for u in range(2)]
 
-        def second_half(s, pieces):
-            part = [interleave(raw, c0, "x_g%d_1_%d" % (s, u)) for u, (raw, c0) in enumerate(pieces)]
-            return [quantize(part[u], "x%d1_%d" % (s, u)) for u in range(2)]
-
-        w_q, x_q = first_half(0, x00, w_raw0)
+        part = [interleave(x00, u * MM_N, "x_g0_0_%d" % u) for u in range(2)]
+        w_g = interleave(w_raw0, 0, "w_g0")
+        x_q = [quantize(part[0], "x00_0")]
+        w_q0 = quantize(w_g, "w0")
+        x_q.append(quantize(part[1], "x00_1"))
         nc.vector.transpose(out=b_cols[:], in_=b_rows[:])
-        finish(0, w_q, x_q, 0)
-        finish(0, w_q, second_half(0, [(x01, 0), (x01, MM_N)]), 1)
-        w_q, x_q = first_half(1, x10, w_raw1)
-        finish(1, w_q, x_q, 0)
-        finish(1, w_q, second_half(1, [(x11a, 0), (x11b, 0)]), 1)
+        finish(0, w_q0, x_q, 0, first_store=1)
+        finish(0, w_q0, pair(0, 1, [(x01, 0), (x01, MM_N)]), 1)
+
+        w_g = interleave(w_raw1, 0, "w_g1")
+        first = interleave(x1[0], 0, "x_g1_0_0")
+        w_q1 = quantize(w_g, "w1")
+        second = interleave(x1[1], 0, "x_g1_0_1")
+        finish(1, w_q1, [quantize(first, "x10_0"), quantize(second, "x10_1")], 0)
+        finish(1, w_q1, pair(1, 1, [(x1[2], 0), (x1[3], 0)]), 1)

@@ -113,22 +113,23 @@ def tile_rows_glin_silu_bias_kernel(tc, x, w, b, out):
                 if c >= first_store:
                     store(s, c if c > first_store else 0, c + 1, h * HALF, HALF)
 
-        def pair(s, h, pieces):
-            part = [interleave(raw, c0, "x_g%d_%d_%d" % (s, h, u)) for u, (raw, c0) in enumerate(pieces)]
-            return [quantize(part[u], "x%d%d_%d" % (s, h, u)) for u in range(2)]
-
-        part = [interleave(x00, u * MM_N, "x_g0_0_%d" % u) for u in range(2)]
+        x_g = interleave(x00, 0, "x_g0_0", width=HALF)
         w_g = interleave(w_raw0, 0, "w_g0")
-        x_q = [quantize(part[0], "x00_0")]
+        codes, scales = quantize(x_g, "x00")
         w_q0 = quantize(w_g, "w0")
-        x_q.append(quantize(part[1], "x00_1"))
         nc.vector.transpose(out=b_cols[:], in_=b_rows[:])
-        finish(0, w_q0, x_q, 0, first_store=1)
-        finish(0, w_q0, pair(0, 1, [(x01, 0), (x01, MM_N)]), 1)
+        blocks = [slice(u * MM_N, (u + 1) * MM_N) for u in range(2)]
+        finish(0, w_q0, [(codes[:, cols], scales[:, cols]) for cols in blocks], 0, first_store=1)
 
+        part = [interleave(x01, u * MM_N, "x_g0_1_%d" % u) for u in range(2)]
+        x_q = [quantize(part[0], "x01_0")]
         w_g = interleave(w_raw1, 0, "w_g1")
-        first = interleave(x1[0], 0, "x_g1_0_0")
+        x_q.append(quantize(part[1], "x01_1"))
+        finish(0, w_q0, x_q, 1)
+
+        first = interleave(x1[0], 0, "x_g1_0")
         w_q1 = quantize(w_g, "w1")
-        second = interleave(x1[1], 0, "x_g1_0_1")
+        second = interleave(x1[1], 0, "x_g1_1")
         finish(1, w_q1, [quantize(first, "x10_0"), quantize(second, "x10_1")], 0)
-        finish(1, w_q1, pair(1, 1, [(x1[2], 0), (x1[3], 0)]), 1)
+        part = [interleave(x1[2 + u], 0, "x_g1_%d" % (2 + u)) for u in range(2)]
+        finish(1, w_q1, [quantize(part[u], "x11_%d" % u) for u in range(2)], 1)

@@ -18,9 +18,11 @@ ROWS = D // PACK
 SIDE = P // ROWS
 SETS = G // SIDE
 MM_N = 128
-BLK = 32
 HALF = N // 2
+BLK = 32
 RUN = 4
+DMA_ALIGN = 256
+MX_ALIGN = 64
 
 
 def tile_rows_glin_silu_bias_kernel(tc, x, w, b, out):
@@ -31,22 +33,22 @@ def tile_rows_glin_silu_bias_kernel(tc, x, w, b, out):
         psum = ctx.enter_context(tc.psum_pool(name="psum", bufs=1))
         ctx.enter_context(tc.manual_schedule())
 
-        b_rows = sb.tile([P, BLK], F32, name="b_rows", align_bytes=64)
-        b_cols = sb.tile([P, BLK], F32, name="b_cols", align_bytes=64)
+        b_rows = sb.tile([P, BLK], F32, name="b_rows", align_bytes=MX_ALIGN)
+        b_cols = sb.tile([P, BLK], F32, name="b_cols", align_bytes=MX_ALIGN)
         b_step = BLK // G
         nc.vector.memset(b_rows[:], 0.0)
 
-        def load(src, name, queue=nc.sync):
-            raw = sb.tile([P, PACK, src.shape[2]], F32, name=name, align_bytes=256)
-            queue.dma_start(out=raw[:], in_=src.rearrange("g (p j) n -> (g p) j n", j=PACK))
+        def load(src, name):
+            raw = sb.tile([P, PACK, src.shape[2]], F32, name=name, align_bytes=DMA_ALIGN)
+            nc.sync.dma_start(out=raw[:], in_=src.rearrange("g (p j) n -> (g p) j n", j=PACK))
             return raw
 
-        def load_x(s, n0, width, queue=nc.sync):
-            return load(x[s * SIDE : (s + 1) * SIDE, :, n0 : n0 + width], "x_raw%d_%d" % (s, n0), queue)
+        def load_x(s, n0, width):
+            return load(x[s * SIDE : (s + 1) * SIDE, :, n0 : n0 + width], "x_raw%d_%d" % (s, n0))
 
-        def interleave(raw, c0, name, copy=nc.vector.tensor_copy, width=MM_N):
-            grouped = sb.tile([P, width, PACK], BF16, name=name, align_bytes=64)
-            copy(
+        def interleave(raw, c0, width, name):
+            grouped = sb.tile([P, width, PACK], BF16, name=name, align_bytes=MX_ALIGN)
+            nc.vector.tensor_copy(
                 out=grouped[:].rearrange("p (c i) j -> p c j i", i=RUN),
                 in_=raw[:, :, c0 : c0 + width].rearrange("p j (c i) -> p c j i", i=RUN),
             )
@@ -54,42 +56,46 @@ def tile_rows_glin_silu_bias_kernel(tc, x, w, b, out):
 
         def quantize(grouped, name):
             width = grouped.shape[1]
-            codes = sb.tile([P, width], U32, name=name + "_codes", align_bytes=64)
-            scales = sb.tile([P, width], U8, name=name + "_scales", align_bytes=64)
+            codes = sb.tile([P, width], U32, name=name + "_codes", align_bytes=MX_ALIGN)
+            scales = sb.tile([P, width], U8, name=name + "_scales", align_bytes=MX_ALIGN)
             nc.vector.quantize_mx(
                 out=codes[:].bitcast(FP8X4), scales=scales[:], in_=grouped[:].rearrange("p c j -> p (c j)")
             )
-            return codes, scales
+            return [(codes[:, c0 : c0 + MM_N], scales[:, c0 : c0 + MM_N]) for c0 in range(0, width, MM_N)]
 
         banks = [[psum.tile([P, N], F32, name="bank%d_%d" % (h, c)) for c in range(SIDE)] for h in range(2)]
-        y = [sb.tile([P, SIDE, N], F32, name="y%d" % s, align_bytes=256) for s in range(SETS)]
+        y = [sb.tile([P, SIDE, N], F32, name="y%d" % s, align_bytes=DMA_ALIGN) for s in range(SETS)]
 
-        def multiply(w_q, x_q, c, h, col):
-            rows = slice(c * ROWS, (c + 1) * ROWS)
-            nc.tensor.matmul_mx(
-                out=banks[h][c][:, col : col + MM_N],
-                lhsT=w_q[0][rows, :].bitcast(FP8X4),
-                lhsT_scale=w_q[1][rows, :],
-                rhs=x_q[0][rows, :].bitcast(FP8X4),
-                rhs_scale=x_q[1][rows, :],
-                start=True,
-                stop=True,
-            )
-
-        def activate(s, c, h, col, n0, width):
-            g = s * SIDE + c
-            nc.scalar.activation(
-                out=y[s][:, c, n0 : n0 + width],
-                in_=banks[h][c][:, col : col + width],
-                func=SILU,
-                bias=b_cols[:, g * b_step : g * b_step + 1],
-            )
-
-        def store(s, c_lo, c_hi, n0, width, queue=nc.sync):
-            queue.dma_start(
-                out=out[s * SIDE + c_lo : s * SIDE + c_hi, :, n0 : n0 + width].rearrange("g m n -> m g n"),
-                in_=y[s][:, c_lo:c_hi, n0 : n0 + width],
-            )
+        def finish(s, h, w_q, x_q, first_store):
+            ((w_codes, w_scales),) = w_q
+            for pair in range(0, SIDE, 2):
+                for u, (x_codes, x_scales) in enumerate(x_q):
+                    for c in (pair, pair + 1):
+                        rows = slice(c * ROWS, (c + 1) * ROWS)
+                        nc.tensor.matmul_mx(
+                            out=banks[h][c][:, u * MM_N : (u + 1) * MM_N],
+                            lhsT=w_codes[rows, :].bitcast(FP8X4),
+                            lhsT_scale=w_scales[rows, :],
+                            rhs=x_codes[rows, :].bitcast(FP8X4),
+                            rhs_scale=x_scales[rows, :],
+                            start=True,
+                            stop=True,
+                        )
+            cols = slice(h * HALF, (h + 1) * HALF)
+            for c in range(SIDE):
+                g = s * SIDE + c
+                nc.scalar.activation(
+                    out=y[s][:, c, cols],
+                    in_=banks[h][c][:, 0:HALF],
+                    func=SILU,
+                    bias=b_cols[:, g * b_step : g * b_step + 1],
+                )
+                if c >= first_store:
+                    c_lo = 0 if c == first_store else c
+                    nc.sync.dma_start(
+                        out=out[s * SIDE + c_lo : g + 1, :, cols].rearrange("g m n -> m g n"),
+                        in_=y[s][:, c_lo : c + 1, cols],
+                    )
 
         nc.scalar.dma_start(out=b_rows[0:P:b_step, :], in_=b.rearrange("g (q i) o -> q g (i o)", i=BLK))
 
@@ -98,38 +104,29 @@ def tile_rows_glin_silu_bias_kernel(tc, x, w, b, out):
         nc.vector.memset(warm_in[:], 0.0)
         nc.scalar.activation(out=warm_out[:], in_=warm_in[:], func=SILU)
 
-        x00 = load_x(0, 0, HALF)
-        w_raw0 = load(w[0:SIDE], "w_raw0")
-        x01 = load_x(0, HALF, HALF)
-        w_raw1 = load(w[SIDE:G], "w_raw1")
-        x1 = [load_x(1, u * MM_N, MM_N) for u in range(4)]
+        x0_first = load_x(0, 0, HALF)
+        w0_raw = load(w[0:SIDE], "w_raw0")
+        x0_second = load_x(0, HALF, HALF)
+        w1_raw = load(w[SIDE:G], "w_raw1")
+        x1_blocks = [load_x(1, n0, MM_N) for n0 in range(0, N, MM_N)]
 
-        def finish(s, w_q, x_q, h, first_store=0):
-            for c in range(SIDE):
-                for u in range(2):
-                    multiply(w_q, x_q[u], c, h, u * MM_N)
-            for c in range(SIDE):
-                activate(s, c, h, 0, h * HALF, HALF)
-                if c >= first_store:
-                    store(s, c if c > first_store else 0, c + 1, h * HALF, HALF)
-
-        x_g = interleave(x00, 0, "x_g0_0", width=HALF)
-        w_g = interleave(w_raw0, 0, "w_g0")
-        codes, scales = quantize(x_g, "x00")
-        w_q0 = quantize(w_g, "w0")
+        x_g = interleave(x0_first, 0, HALF, "x_g0_0")
+        w0_g = interleave(w0_raw, 0, M, "w_g0")
+        x_q = quantize(x_g, "x00")
+        w0_q = quantize(w0_g, "w0")
         nc.vector.transpose(out=b_cols[:], in_=b_rows[:])
-        blocks = [slice(u * MM_N, (u + 1) * MM_N) for u in range(2)]
-        finish(0, w_q0, [(codes[:, cols], scales[:, cols]) for cols in blocks], 0, first_store=1)
+        finish(0, 0, w0_q, x_q, first_store=1)
 
-        part = [interleave(x01, u * MM_N, "x_g0_1_%d" % u) for u in range(2)]
-        x_q = [quantize(part[0], "x01_0")]
-        w_g = interleave(w_raw1, 0, "w_g1")
-        x_q.append(quantize(part[1], "x01_1"))
-        finish(0, w_q0, x_q, 1)
+        parts = [interleave(x0_second, u * MM_N, MM_N, "x_g0_1_%d" % u) for u in range(2)]
+        x_q = quantize(parts[0], "x01_0")
+        w1_g = interleave(w1_raw, 0, M, "w_g1")
+        x_q = x_q + quantize(parts[1], "x01_1")
+        finish(0, 1, w0_q, x_q, first_store=0)
 
-        first = interleave(x1[0], 0, "x_g1_0")
-        w_q1 = quantize(w_g, "w1")
-        second = interleave(x1[1], 0, "x_g1_1")
-        finish(1, w_q1, [quantize(first, "x10_0"), quantize(second, "x10_1")], 0)
-        part = [interleave(x1[2 + u], 0, "x_g1_%d" % (2 + u)) for u in range(2)]
-        finish(1, w_q1, [quantize(part[u], "x11_%d" % u) for u in range(2)], 1)
+        parts = [interleave(x1_blocks[0], 0, MM_N, "x_g1_0")]
+        w1_q = quantize(w1_g, "w1")
+        parts.append(interleave(x1_blocks[1], 0, MM_N, "x_g1_1"))
+        finish(1, 0, w1_q, quantize(parts[0], "x10_0") + quantize(parts[1], "x10_1"), first_store=0)
+
+        parts = [interleave(x1_blocks[u], 0, MM_N, "x_g1_%d" % u) for u in (2, 3)]
+        finish(1, 1, w1_q, quantize(parts[0], "x11_0") + quantize(parts[1], "x11_1"), first_store=0)

@@ -46,12 +46,15 @@ def tile_rows_glin_silu_bias_kernel(tc, x, w, b, out):
         def load_x(s, n0, width):
             return load(x[s * SIDE : (s + 1) * SIDE, :, n0 : n0 + width], "x_raw%d_%d" % (s, n0))
 
-        def interleave(raw, c0, width, name):
+        def interleave(raw, c0, width, name, on_scalar=0):
             grouped = sb.tile([P, width, PACK], BF16, name=name, align_bytes=MX_ALIGN)
-            nc.vector.tensor_copy(
-                out=grouped[:].rearrange("p (c i) j -> p c j i", i=RUN),
-                in_=raw[:, :, c0 : c0 + width].rearrange("p j (c i) -> p c j i", i=RUN),
-            )
+            cut = width - on_scalar
+            for copy, lo, hi in ((nc.vector.tensor_copy, 0, cut), (nc.scalar.copy, cut, width)):
+                if hi > lo:
+                    copy(
+                        out=grouped[:, lo:hi, :].rearrange("p (c i) j -> p c j i", i=RUN),
+                        in_=raw[:, :, c0 + lo : c0 + hi].rearrange("p j (c i) -> p c j i", i=RUN),
+                    )
             return grouped
 
         def quantize(grouped, name):
@@ -110,8 +113,8 @@ def tile_rows_glin_silu_bias_kernel(tc, x, w, b, out):
         w1_raw = load(w[SIDE:G], "w_raw1")
         x1_blocks = [load_x(1, n0, MM_N) for n0 in range(0, N, MM_N)]
 
-        x_g = interleave(x0_first, 0, HALF, "x_g0_0")
-        w0_g = interleave(w0_raw, 0, M, "w_g0")
+        x_g = interleave(x0_first, 0, HALF, "x_g0_0", on_scalar=64)
+        w0_g = interleave(w0_raw, 0, M, "w_g0", on_scalar=40)
         x_q = quantize(x_g, "x00")
         w0_q = quantize(w0_g, "w0")
         nc.vector.transpose(out=b_cols[:], in_=b_rows[:])

@@ -57,48 +57,61 @@ def tile_rows_glin_silu_bias_kernel(tc, x, w, b, out):
                     )
             return grouped
 
-        def quantize(grouped, name):
-            width = grouped.shape[1]
+        def operand(width, name):
             codes = sb.tile([P, width], U32, name=name + "_codes", align_bytes=MX_ALIGN)
             scales = sb.tile([P, width], U8, name=name + "_scales", align_bytes=MX_ALIGN)
-            nc.vector.quantize_mx(
-                out=codes[:].bitcast(FP8X4), scales=scales[:], in_=grouped[:].rearrange("p c j -> p (c j)")
-            )
-            return [(codes[:, c0 : c0 + MM_N], scales[:, c0 : c0 + MM_N]) for c0 in range(0, width, MM_N)]
+            return codes, scales
 
-        banks = [[psum.tile([P, N], F32, name="bank%d_%d" % (h, c)) for c in range(SIDE)] for h in range(2)]
+        def quantize(grouped, into, c0):
+            cols = slice(c0, c0 + grouped.shape[1])
+            nc.vector.quantize_mx(
+                out=into[0][:, cols].bitcast(FP8X4),
+                scales=into[1][:, cols],
+                in_=grouped[:].rearrange("p c j -> p (c j)"),
+            )
+
+        def copy_halves(raw, name, on_scalar=0):
+            return [
+                interleave(raw, k * MM_N // 2, MM_N // 2, "%s_%d" % (name, k), on_scalar * k) for k in range(2)
+            ]
+
+        def quantize_halves(halves, into, c0):
+            for k in range(2):
+                quantize(halves[k], into, c0 + k * MM_N // 2)
+
+        def prepare_in_halves(raw, into, c0, name):
+            quantize_halves(copy_halves(raw, name), into, c0)
+
+        w_q = [operand(M, "w%d" % s) for s in range(SETS)]
+        x_q = [operand(N, "x%d" % s) for s in range(SETS)]
+        banks = [[psum.tile([P, N], F32, name="bank%d_%d" % (k, c)) for c in range(SIDE)] for k in range(2)]
         y = [sb.tile([P, SIDE, N], F32, name="y%d" % s, align_bytes=DMA_ALIGN) for s in range(SETS)]
 
-        def finish(s, h, w_q, x_q, first_store):
-            ((w_codes, w_scales),) = w_q
-            for pair in range(0, SIDE, 2):
-                for u, (x_codes, x_scales) in enumerate(x_q):
-                    for c in (pair, pair + 1):
-                        rows = slice(c * ROWS, (c + 1) * ROWS)
-                        nc.tensor.matmul_mx(
-                            out=banks[h][c][:, u * MM_N : (u + 1) * MM_N],
-                            lhsT=w_codes[rows, :].bitcast(FP8X4),
-                            lhsT_scale=w_scales[rows, :],
-                            rhs=x_codes[rows, :].bitcast(FP8X4),
-                            rhs_scale=x_scales[rows, :],
-                            start=True,
-                            stop=True,
-                        )
-            cols = slice(h * HALF, (h + 1) * HALF)
-            for c in range(SIDE):
-                g = s * SIDE + c
-                nc.scalar.activation(
-                    out=y[s][:, c, cols],
-                    in_=banks[h][c][:, 0:HALF],
-                    func=SILU,
-                    bias=b_cols[:, g * b_step : g * b_step + 1],
-                )
-                if c >= first_store:
-                    c_lo = 0 if c == first_store else c
-                    nc.sync.dma_start(
-                        out=out[s * SIDE + c_lo : g + 1, :, cols].rearrange("g m n -> m g n"),
-                        in_=y[s][:, c_lo : c + 1, cols],
-                    )
+        def multiply(s, c, u, bank):
+            rows = slice(c * ROWS, (c + 1) * ROWS)
+            cols = slice(u * MM_N, (u + 1) * MM_N)
+            nc.tensor.matmul_mx(
+                out=banks[bank][c][:, cols],
+                lhsT=w_q[s][0][rows, :].bitcast(FP8X4),
+                lhsT_scale=w_q[s][1][rows, :],
+                rhs=x_q[s][0][rows, cols].bitcast(FP8X4),
+                rhs_scale=x_q[s][1][rows, cols],
+                start=True,
+                stop=True,
+            )
+
+        def activate(s, c, u0, u1, bank):
+            g = s * SIDE + c
+            cols = slice(u0 * MM_N, u1 * MM_N)
+            nc.scalar.activation(
+                out=y[s][:, c, cols], in_=banks[bank][c][:, cols], func=SILU, bias=b_cols[:, g * b_step : g * b_step + 1]
+            )
+
+        def store(s, c0, c1, u0, u1):
+            cols = slice(u0 * MM_N, u1 * MM_N)
+            nc.sync.dma_start(
+                out=out[s * SIDE + c0 : s * SIDE + c1, :, cols].rearrange("g m n -> m g n"), in_=y[s][:, c0:c1, cols]
+            )
 
         nc.scalar.dma_start(out=b_rows[0:P:b_step, :], in_=b.rearrange("g (q i) o -> q g (i o)", i=BLK))
 
@@ -106,6 +119,25 @@ def tile_rows_glin_silu_bias_kernel(tc, x, w, b, out):
         warm_out = sb.tile([P, 1], F32, name="warm_out")
         nc.vector.memset(warm_in[:], 0.0)
         nc.scalar.activation(out=warm_out[:], in_=warm_in[:], func=SILU)
+
+        def multiply_half(s, h, pairs):
+            for pair in pairs:
+                for u in (2 * h, 2 * h + 1):
+                    for c in pair:
+                        multiply(s, c, u, h)
+
+        def finish_half(s, h):
+            cols = slice(h * HALF, (h + 1) * HALF)
+            for c in range(SIDE):
+                g = s * SIDE + c
+                nc.scalar.activation(
+                    out=y[s][:, c, cols],
+                    in_=banks[h][c][:, cols],
+                    func=SILU,
+                    bias=b_cols[:, g * b_step : g * b_step + 1],
+                )
+                if (s, h, c) != (0, 0, 0):
+                    store(s, 0 if (s, h, c) == (0, 0, 1) else c, c + 1, 2 * h, 2 * h + 2)
 
         x0_first = load_x(0, 0, HALF)
         w0_raw = load(w[0:SIDE], "w_raw0")
@@ -115,21 +147,29 @@ def tile_rows_glin_silu_bias_kernel(tc, x, w, b, out):
 
         x_g = interleave(x0_first, 0, HALF, "x_g0_0", on_scalar=64)
         w0_g = interleave(w0_raw, 0, M, "w_g0", on_scalar=40)
-        x_q = quantize(x_g, "x00")
-        w0_q = quantize(w0_g, "w0")
+        quantize(x_g, x_q[0], 0)
+        quantize(w0_g, w_q[0], 0)
         nc.vector.transpose(out=b_cols[:], in_=b_rows[:])
-        finish(0, 0, w0_q, x_q, first_store=1)
+        multiply_half(0, 0, ((0, 1), (2, 3)))
+        finish_half(0, 0)
 
         parts = [interleave(x0_second, u * MM_N, MM_N, "x_g0_1_%d" % u) for u in range(2)]
-        x_q = quantize(parts[0], "x01_0")
+        quantize(parts[0], x_q[0], HALF)
         w1_g = interleave(w1_raw, 0, M, "w_g1")
-        x_q = x_q + quantize(parts[1], "x01_1")
-        finish(0, 1, w0_q, x_q, first_store=0)
+        quantize(parts[1], x_q[0], HALF + MM_N)
+        multiply_half(0, 1, ((0, 1), (2, 3)))
+        finish_half(0, 1)
 
-        parts = [interleave(x1_blocks[0], 0, MM_N, "x_g1_0")]
-        w1_q = quantize(w1_g, "w1")
-        parts.append(interleave(x1_blocks[1], 0, MM_N, "x_g1_1"))
-        finish(1, 0, w1_q, quantize(parts[0], "x10_0") + quantize(parts[1], "x10_1"), first_store=0)
-
-        parts = [interleave(x1_blocks[u], 0, MM_N, "x_g1_%d" % u) for u in (2, 3)]
-        finish(1, 1, w1_q, quantize(parts[0], "x11_0") + quantize(parts[1], "x11_1"), first_store=0)
+        first = interleave(x1_blocks[0], 0, MM_N, "x_g1_0")
+        quantize(w1_g, w_q[1], 0)
+        second = copy_halves(x1_blocks[1], "x_g1_1")
+        quantize(first, x_q[1], 0)
+        quantize_halves(second, x_q[1], MM_N)
+        multiply_half(1, 0, ((0, 1), (2, 3)))
+        first = interleave(x1_blocks[2], 0, MM_N, "x_g1_2")
+        second = copy_halves(x1_blocks[3], "x_g1_3")
+        quantize(first, x_q[1], HALF)
+        quantize_halves(second, x_q[1], HALF + MM_N)
+        finish_half(1, 0)
+        multiply_half(1, 1, ((0, 1), (2, 3)))
+        finish_half(1, 1)

@@ -146,10 +146,10 @@ def tile_rows_glin_silu_bias_kernel(tc, x, w, b, out):
         x1_blocks = [load_x(1, n0, MM_N) for n0 in range(0, N, MM_N)]
 
         x_g = interleave(x0_first, 0, HALF, "x_g0_0", on_scalar=64)
-        w0_g = interleave(w0_raw, 0, M, "w_g0", on_scalar=40)
+        nc.vector.transpose(out=b_cols[:], in_=b_rows[:])
+        w0_g = interleave(w0_raw, 0, M, "w_g0", on_scalar=24)
         quantize(x_g, x_q[0], 0)
         quantize(w0_g, w_q[0], 0)
-        nc.vector.transpose(out=b_cols[:], in_=b_rows[:])
         multiply_half(0, 0, ((0, 1), (2, 3)))
         finish_half(0, 0)
 

from contextlib import ExitStack

import concourse.mybir as mybir

G, D, M, N = 8, 128, 128, 512
FLOPS = 2 * G * D * M * N

F32 = mybir.dt.float32
BF16 = mybir.dt.bfloat16
U32 = mybir.dt.uint32
U8 = mybir.dt.uint8
FP8X4 = mybir.dt.float8_e4m3fn_x4
SILU = mybir.ActivationFunctionType.Silu

P = 128
PACK = 4
ROWS = D // PACK
SIDE = P // ROWS
SETS = G // SIDE
MM_N = 128
HALF = N // 2
BLK = 32
RUN = 4
DMA_ALIGN = 256
MX_ALIGN = 64


def tile_rows_glin_silu_bias_kernel(tc, x, w, b, out):
    nc = tc.nc

    with ExitStack() as ctx:
        sb = ctx.enter_context(tc.tile_pool(name="sb", bufs=1))
        psum = ctx.enter_context(tc.psum_pool(name="psum", bufs=1))
        ctx.enter_context(tc.manual_schedule())

        b_rows = sb.tile([P, BLK], F32, name="b_rows", align_bytes=MX_ALIGN)
        b_cols = sb.tile([P, BLK], F32, name="b_cols", align_bytes=MX_ALIGN)
        b_step = BLK // G
        nc.vector.memset(b_rows[:], 0.0)

        def load(src, name):
            raw = sb.tile([P, PACK, src.shape[2]], F32, name=name, align_bytes=DMA_ALIGN)
            nc.sync.dma_start(out=raw[:], in_=src.rearrange("g (p j) n -> (g p) j n", j=PACK))
            return raw

        def load_x(s, n0, width):
            return load(x[s * SIDE : (s + 1) * SIDE, :, n0 : n0 + width], "x_raw%d_%d" % (s, n0))

        def interleave(raw, c0, width, name, on_scalar=0):
            grouped = sb.tile([P, width, PACK], BF16, name=name, align_bytes=MX_ALIGN)
            cut = width - on_scalar
            for copy, lo, hi in ((nc.vector.tensor_copy, 0, cut), (nc.scalar.copy, cut, width)):
                if hi > lo:
                    copy(
                        out=grouped[:, lo:hi, :].rearrange("p (c i) j -> p c j i", i=RUN),
                        in_=raw[:, :, c0 + lo : c0 + hi].rearrange("p j (c i) -> p c j i", i=RUN),
                    )
            return grouped

        def operand(width, name):
            codes = sb.tile([P, width], U32, name=name + "_codes", align_bytes=MX_ALIGN)
            scales = sb.tile([P, width], U8, name=name + "_scales", align_bytes=MX_ALIGN)
            return codes, scales

        def quantize(grouped, into, c0):
            cols = slice(c0, c0 + grouped.shape[1])
            nc.vector.quantize_mx(
                out=into[0][:, cols].bitcast(FP8X4),
                scales=into[1][:, cols],
                in_=grouped[:].rearrange("p c j -> p (c j)"),
            )

        def copy_halves(raw, name, on_scalar=0):
            return [
                interleave(raw, k * MM_N // 2, MM_N // 2, "%s_%d" % (name, k), on_scalar * k) for k in range(2)
            ]

        def quantize_halves(halves, into, c0):
            for k in range(2):
                quantize(halves[k], into, c0 + k * MM_N // 2)

        def prepare_in_halves(raw, into, c0, name):
            quantize_halves(copy_halves(raw, name), into, c0)

        w_q = [operand(M, "w%d" % s) for s in range(SETS)]
        x_q = [operand(N, "x%d" % s) for s in range(SETS)]
        banks = [[psum.tile([P, N], F32, name="bank%d_%d" % (k, c)) for c in range(SIDE)] for k in range(2)]
        y = [sb.tile([P, SIDE, N], F32, name="y%d" % s, align_bytes=DMA_ALIGN) for s in range(SETS)]

        def multiply(s, c, u, bank):
            rows = slice(c * ROWS, (c + 1) * ROWS)
            cols = slice(u * MM_N, (u + 1) * MM_N)
            nc.tensor.matmul_mx(
                out=banks[bank][c][:, cols],
                lhsT=w_q[s][0][rows, :].bitcast(FP8X4),
                lhsT_scale=w_q[s][1][rows, :],
                rhs=x_q[s][0][rows, cols].bitcast(FP8X4),
                rhs_scale=x_q[s][1][rows, cols],
                start=True,
                stop=True,
            )

        def activate(s, c, u0, u1, bank):
            g = s * SIDE + c
            cols = slice(u0 * MM_N, u1 * MM_N)
            nc.scalar.activation(
                out=y[s][:, c, cols], in_=banks[bank][c][:, cols], func=SILU, bias=b_cols[:, g * b_step : g * b_step + 1]
            )

        def store(s, c0, c1, u0, u1):
            cols = slice(u0 * MM_N, u1 * MM_N)
            nc.sync.dma_start(
                out=out[s * SIDE + c0 : s * SIDE + c1, :, cols].rearrange("g m n -> m g n"), in_=y[s][:, c0:c1, cols]
            )

        nc.scalar.dma_start(out=b_rows[0:P:b_step, :], in_=b.rearrange("g (q i) o -> q g (i o)", i=BLK))

        warm_in = sb.tile([P, 1], F32, name="warm_in")
        warm_out = sb.tile([P, 1], F32, name="warm_out")
        nc.vector.memset(warm_in[:], 0.0)
        nc.scalar.activation(out=warm_out[:], in_=warm_in[:], func=SILU)

        def multiply_half(s, h, pairs):
            for pair in pairs:
                for u in (2 * h, 2 * h + 1):
                    for c in pair:
                        multiply(s, c, u, h)

        def finish_half(s, h):
            cols = slice(h * HALF, (h + 1) * HALF)
            for c in range(SIDE):
                g = s * SIDE + c
                nc.scalar.activation(
                    out=y[s][:, c, cols],
                    in_=banks[h][c][:, cols],
                    func=SILU,
                    bias=b_cols[:, g * b_step : g * b_step + 1],
                )
                if (s, h, c) != (0, 0, 0):
                    store(s, 0 if (s, h, c) == (0, 0, 1) else c, c + 1, 2 * h, 2 * h + 2)

        x0_first = load_x(0, 0, HALF)
        w0_raw = load(w[0:SIDE], "w_raw0")
        x0_second = load_x(0, HALF, HALF)
        w1_raw = load(w[SIDE:G], "w_raw1")
        x1_blocks = [load_x(1, n0, MM_N) for n0 in range(0, N, MM_N)]

        x_g = interleave(x0_first, 0, HALF, "x_g0_0", on_scalar=64)
        nc.vector.transpose(out=b_cols[:], in_=b_rows[:])
        w0_g = interleave(w0_raw, 0, M, "w_g0", on_scalar=24)
        quantize(x_g, x_q[0], 0)
        quantize(w0_g, w_q[0], 0)
        multiply_half(0, 0, ((0, 1), (2, 3)))
        finish_half(0, 0)

        parts = [interleave(x0_second, u * MM_N, MM_N, "x_g0_1_%d" % u) for u in range(2)]
        quantize(parts[0], x_q[0], HALF)
        w1_g = interleave(w1_raw, 0, M, "w_g1")
        quantize(parts[1], x_q[0], HALF + MM_N)
        multiply_half(0, 1, ((0, 1), (2, 3)))
        finish_half(0, 1)

        first = interleave(x1_blocks[0], 0, MM_N, "x_g1_0")
        quantize(w1_g, w_q[1], 0)
        second = copy_halves(x1_blocks[1], "x_g1_1")
        quantize(first, x_q[1], 0)
        quantize_halves(second, x_q[1], MM_N)
        multiply_half(1, 0, ((0, 1), (2, 3)))
        first = interleave(x1_blocks[2], 0, MM_N, "x_g1_2")
        second = copy_halves(x1_blocks[3], "x_g1_3")
        quantize(first, x_q[1], HALF)
        quantize_halves(second, x_q[1], HALF + MM_N)
        finish_half(1, 0)
        multiply_half(1, 1, ((0, 1), (2, 3)))
        finish_half(1, 1)
